import numpy as np
import ml_dtypes


def mxq(x, axis, fmt="e4m3"):
    dtype, down = {"e4m3": (ml_dtypes.float8_e4m3fn, 7), "e5m2": (ml_dtypes.float8_e5m2, 14)}[fmt]
    v = np.moveaxis(np.asarray(x, np.float32).astype(ml_dtypes.bfloat16).astype(np.float64), axis, -1)
    blocks = v.reshape(v.shape[:-1] + (-1, 32))
    amax = np.abs(blocks).max(-1, keepdims=True)
    byte = np.maximum(np.where(amax > 0, np.frexp(amax)[1] - 1 + 127, 0) - down, 1)
    scale = np.exp2(byte - 127.0)
    codes = (blocks / scale).astype(np.float32).astype(dtype).astype(np.float64)
    return np.moveaxis((codes * scale).reshape(v.shape), -1, axis)


WIDE = False


def mx_kscale(k):
    if not WIDE:
        return np.ones(k)
    levels = np.array([10, -10, 5, -5, 0])
    if k % 512:
        return np.exp2(np.random.permutation(np.resize(levels, k // 32))).repeat(32)
    a = np.empty((k // 512, 16))
    for p in range(k // 512):
        a[p, :8] = np.random.permutation(np.resize(levels, 8))
        for g in range(8):
            far = levels[np.abs(levels - a[p, g]) >= 10]
            a[p, g + 8] = far[np.random.randint(len(far))]
    return np.exp2(a.ravel()).repeat(32)


def f64(x):
    return np.asarray(x).astype(np.float64)


def striped(idx):
    return np.tile(idx.reshape(-1, 16).T, (8, 1)).astype(np.uint16)


def unstriped(offs):
    return offs[:16].T.reshape(-1).astype(np.int64)


def striped8(idx):
    return np.concatenate([x.reshape(-1, 16).T for x in idx]).astype(np.uint16)


def runs(offs, k):
    lists = np.stack([offs[16 * r : 16 * r + 16].T.reshape(-1) for r in range(8)]).astype(np.int64)
    return lists[np.arange(k) % 512 // 64]


def pack_weight(w):
    k, n = w.shape
    w = f64(np.asarray(w, np.float32).astype(ml_dtypes.bfloat16)).reshape(k // 32, 32, n)
    amax = np.abs(w).max(1)
    byte = np.clip(np.where(amax > 0, np.frexp(amax)[1] - 1 + 127 - 7, 1), 1, 254)
    scaled = (w * np.exp2(127.0 - byte)[:, None, :]).reshape(k, n).astype(np.float32)
    words = np.ascontiguousarray(scaled.reshape(k // 512, 128, 4, n).transpose(0, 1, 3, 2)).astype(ml_dtypes.float8_e4m3fn).view(np.uint8)
    return words, np.ascontiguousarray(byte.astype(np.uint8).reshape(k // 512, 16, n))


def unpack_weight(words, scales):
    g, p, n, _ = words.shape
    vals = np.ascontiguousarray(words).view(ml_dtypes.float8_e4m3fn).astype(np.float64) * np.repeat(np.exp2(scales.astype(np.float64) - 127.0), 8, axis=1)[..., None]
    return vals.transpose(0, 1, 3, 2).reshape(g * 512, n)


K, T, S, H, G = 512, 2048, 256, 512, 2048


def setup_inputs():
    n = np.random.standard_normal
    s = mx_kscale(K)[:, None]
    packed_xT = pack_weight(n((K, T)) * s)
    packed_dT = pack_weight(n((K, G)) / s)
    return {
        "x_words": packed_xT[0],
        "x_scales": packed_xT[1],
        "w1": (n((K, H)) / np.sqrt(K) / s).astype(np.float32),
        "gs": (np.random.uniform(0.5, 1.5, (K, 1)) * s).astype(np.float32),
        "d_words": packed_dT[0],
        "d_scales": packed_dT[1],
        "offs": striped(np.random.permutation(T)[:S]),
        "ka": striped8(np.random.randint(0, G, (8, H))),
        "kb": striped8(np.random.randint(0, G, (8, H))),
        "n1": striped(np.random.permutation(S)),
        "n2": striped(np.random.permutation(S)),
    }


def reference(x_words, x_scales, w1, gs, d_words, d_scales, offs, ka, kb, n1, n2):
    d_ka = unpack_weight(d_words, d_scales)[np.arange(K)[:, None], runs(ka, K)]
    xq = unpack_weight(x_words, x_scales)[:, unstriped(offs)]
    y = mxq(f64(w1), 0, "e4m3").T @ xq
    z = f64(gs) * y
    zq = mxq(z, 0, "e4m3")
    d_kb = unpack_weight(d_words, d_scales)[np.arange(K)[:, None], runs(kb, K)]
    h = 0.0625 * (d_ka.T @ zq + d_kb.T @ zq)
    ds = np.zeros((H, S))
    ds[:, unstriped(n1)] = h
    ds2 = np.zeros((H, S))
    ds2[:, unstriped(n2)] = h
    return np.maximum(ds, ds2)

@@ -1,0 +1,178 @@
+from contextlib import ExitStack
+
+import concourse.mybir as mybir
+
+K, T, S, H, G = 512, 2048, 256, 512, 2048
+FLOPS = 2 * K * H * S * 3
+
+F32 = mybir.dt.float32
+BF16 = mybir.dt.bfloat16
+I32 = mybir.dt.int32
+U32 = mybir.dt.uint32
+U16 = mybir.dt.uint16
+U8 = mybir.dt.uint8
+FP8X4 = mybir.dt.float8_e4m3fn_x4
+MULT = mybir.AluOpType.mult
+MAX = mybir.AluOpType.max
+COPY = mybir.ActivationFunctionType.Copy
+
+P = 128
+PACK = 4
+LIST = 16
+HALF = S // 2
+PICK = 256
+WIDE = 2 * S
+
+
+def tile_picked_daqisendtwo_none_p_kernel(
+    tc, x_words, x_scales, w1, gs, d_words, d_scales, offs, ka, kb, n1, n2, out
+):
+    nc = tc.nc
+    with ExitStack() as ctx:
+        keep = ctx.enter_context(tc.tile_pool(name="keep", bufs=1))
+        reuse = ctx.enter_context(tc.tile_pool(name="reuse", bufs=1))
+        psum = ctx.enter_context(tc.psum_pool(name="psum", bufs=1))
+
+        def sb(name, shape, dtype):
+            return keep.tile(shape, dtype, name=name, align_bytes=64)
+
+        def placed(name, shape, dtype, at):
+            return reuse.tile(shape, dtype, name=name, align_bytes=64, offset=at)
+
+        def entries(tile, first, count):
+            return tile[:, first // LIST : (first + count) // LIST]
+
+        ka_sb = sb("ka_sb", [P, H // LIST], U16)
+        kb_sb = sb("kb_sb", [P, H // LIST], U16)
+        offs_sb = sb("offs_sb", [P, S // LIST], U16)
+        n1_sb = sb("n1_sb", [P, S // LIST], U16)
+        n2_sb = sb("n2_sb", [P, S // LIST], U16)
+        ds_tab = sb("ds_tab", [P, G], U8)
+        xs_tab = placed("xs_tab", [P, T], U8, 0)
+        dw_tab = sb("dw_tab", [P, G], U32)
+        xw_tab = sb("xw_tab", [P, T], U32)
+        w_raw = sb("w_raw", [P, PACK, H], F32)
+        gs_sb = sb("gs_sb", [P, PACK], F32)
+
+        d_plane = sb("d_plane", [P, 2, H], U8)
+        d_plane_i = d_plane[:].rearrange("p a n -> p (a n)").bitcast(I32)
+        nc.vector.memset(ds_tab[:].bitcast(I32), 0)
+        nc.vector.memset(xs_tab[:].bitcast(I32), 0)
+        nc.vector.memset(d_plane_i, 0)
+
+        w_rows = w1.rearrange("(p j) c -> p j c", j=PACK)
+        nc.sync.dma_start(ka_sb[:], ka)
+        nc.sync.dma_start(kb_sb[:], kb)
+        nc.sync.dma_start(w_raw[:, 0:2, :], w_rows[:, 0:2, :])
+        nc.scalar.dma_start(ds_tab[0:P:8, :].bitcast(I32), d_scales[0].bitcast(I32))
+        nc.sync.dma_start(offs_sb[:], offs)
+        nc.sync.dma_start(w_raw[:, 2:4, :], w_rows[:, 2:4, :])
+        for i in range(4):
+            nc.scalar.dma_start(xs_tab[i:P:32, :].bitcast(I32), x_scales[0, i:16:4, :].bitcast(I32))
+        nc.sync.dma_start(xw_tab[:].bitcast(I32), x_words[0].rearrange("p n t -> p (n t)").bitcast(I32))
+        nc.sync.dma_start(dw_tab[:].bitcast(I32), d_words[0].rearrange("p n t -> p (n t)").bitcast(I32))
+        nc.gpsimd.dma_start(gs_sb[:], gs.rearrange("(p t) o -> p (t o)", t=PACK))
+        nc.sync.dma_start(n1_sb[:], n1)
+        nc.sync.dma_start(n2_sb[:], n2)
+
+        ds_pick = sb("ds_pick", [P, 2, H], U8)
+        for a, codes in enumerate((ka_sb, kb_sb)):
+            nc.vector.tensor_copy(ds_pick[:, a, :], ds_tab[:].indirect(codes[:]))
+        ds_pick_i = ds_pick[:].rearrange("p a n -> p (a n)").bitcast(I32)
+        for i in range(4):
+            nc.sync.dma_start(d_plane_i[i:P:32, :], ds_pick_i[8 * i : P : 32, :])
+
+        d_code = {}
+
+        def pick_d_words(c):
+            for a, codes in enumerate((ka_sb, kb_sb)):
+                d_code[c, a] = placed(f"d_code{c}{a}", [P, PICK], U32, 2048 + 1024 * a)
+                nc.vector.tensor_copy(d_code[c, a][:], dw_tab[:].indirect(entries(codes, c * PICK, PICK)))
+
+        w_view = w_raw[:].rearrange("p j (m t) -> p m t j", t=PACK)
+        w_code, w_plane = [], []
+        w_bf = [sb(f"w_bf{u}", [P, 2, P, PACK], BF16) for u in range(2)]
+        nc.scalar.activation(w_bf[0][:].rearrange("p t m j -> p m t j"), w_view[:, :, 0:2, :], COPY)
+        nc.vector.tensor_copy(w_bf[1][:].rearrange("p t m j -> p m t j"), w_view[:, :, 2:4, :])
+        x_plane = sb("x_plane", [P, S], U8)
+        nc.vector.tensor_copy(x_plane[:], xs_tab[:].indirect(offs_sb[:]))
+        for u in (1, 0):
+            code = sb(f"w_code{u}", [P, 2 * P], U32)
+            plane = sb(f"w_plane{u}", [P, 2 * P], U8)
+            nc.vector.quantize_mx(code[:].bitcast(FP8X4), plane[:], w_bf[u][:].rearrange("p t m j -> p (t m j)"))
+            w_code.insert(0, code)
+            w_plane.insert(0, plane)
+
+        z_code = sb("z_code", [P, S], U32)
+        z_plane = sb("z_plane", [P, S], U8)
+
+        x_codes = []
+        for b in range(2):
+            x_codes.append(placed(f"x_code{b}", [P, HALF], U32, 512 * b))
+            nc.vector.tensor_copy(x_codes[b][:], xw_tab[:].indirect(entries(offs_sb, b * HALF, HALF)))
+
+        def first_layer(b):
+            cols = slice(b * HALF, (b + 1) * HALF)
+            x_code = x_codes[b]
+            y = psum.tile([P, PACK, HALF], F32, name=f"y{b}", tag=f"bank_y{b}")
+            for t in range(PACK):
+                m = slice((t % 2) * P, (t % 2 + 1) * P)
+                nc.tensor.matmul_mx(
+                    y[:, t, :],
+                    lhsT=w_code[t // 2][:, m].bitcast(FP8X4),
+                    lhsT_scale=w_plane[t // 2][:, m],
+                    rhs=x_code[:].bitcast(FP8X4),
+                    rhs_scale=x_plane[:, cols],
+                    start=True,
+                    stop=True,
+                )
+            z_bf = placed(f"z_bf{b}", [P, HALF, PACK], BF16, (2048 + 512, 4096)[b])
+            nc.vector.tensor_tensor(
+                z_bf[:],
+                y[:].rearrange("p t n -> p n t"),
+                gs_sb[:].unsqueeze(1).to_broadcast([P, HALF, PACK]),
+                MULT,
+            )
+            nc.vector.quantize_mx(z_code[:, cols].bitcast(FP8X4), z_plane[:, cols], z_bf[:].rearrange("p n t -> p (n t)"))
+
+        h_sb = [sb(f"h_sb{r}", [P, S], F32) for r in range(4)]
+        sent = [[sb(f"sent{r}{a}", [P, WIDE], F32) for a in range(2)] for r in range(4)]
+
+        def second_layer(r, first, count):
+            cols = slice(first, first + count)
+            c, m = r // 2, slice((r % 2) * P, (r % 2 + 1) * P)
+            tag = "bank_y1" if (r, first) == (0, 0) else f"bank{r}_{first}"
+            acc = psum.tile([P, count], F32, name=f"acc{r}_{first}", tag=tag)
+            for a in range(2):
+                nc.tensor.matmul_mx(
+                    acc[:],
+                    lhsT=d_code[c, a][:, m].bitcast(FP8X4),
+                    lhsT_scale=d_plane[:, a, r * P : (r + 1) * P],
+                    rhs=z_code[:, cols].bitcast(FP8X4),
+                    rhs_scale=z_plane[:, cols],
+                    start=(a == 0),
+                    stop=(a == 1),
+                )
+            nc.vector.tensor_scalar_mul(h_sb[r][:, cols], acc[:], 0.0625)
+            for a, places in enumerate((n1_sb, n2_sb)):
+                nc.scalar.activation(sent[r][a][:].indirect(entries(places, first, count)), h_sb[r][:, cols], COPY)
+
+        def finish(r):
+            res = sb(f"res{r}", [P, S], F32)
+            nc.vector.tensor_tensor(res[:], sent[r][0][:, :S], sent[r][1][:, :S], MAX)
+            nc.sync.dma_start(out[r * P : (r + 1) * P, :], res[:])
+
+        first_layer(0)
+        pick_d_words(0)
+        second_layer(0, 0, HALF)
+        second_layer(1, 0, HALF)
+        first_layer(1)
+        second_layer(0, HALF, HALF)
+        second_layer(1, HALF, HALF)
+        pick_d_words(1)
+        finish(0)
+        second_layer(2, 0, S)
+        finish(1)
+        second_layer(3, 0, S)
+        finish(2)
+        finish(3)

@@ -13,6 +13,7 @@ U16 = mybir.dt.uint16
 U8 = mybir.dt.uint8
 FP8X4 = mybir.dt.float8_e4m3fn_x4
 MULT = mybir.AluOpType.mult
+ADD = mybir.AluOpType.add
 MAX = mybir.AluOpType.max
 COPY = mybir.ActivationFunctionType.Copy
 
@@ -48,8 +49,8 @@ def tile_picked_daqisendtwo_none_p_kernel(
         n1_sb = sb("n1_sb", [P, S // LIST], U16)
         n2_sb = sb("n2_sb", [P, S // LIST], U16)
         ds_tab = sb("ds_tab", [P, G], U8)
-        xs_tab = placed("xs_tab", [P, T], U8, 0)
         dw_tab = sb("dw_tab", [P, G], U32)
+        xs_tab = placed("xs_tab", [P, T], U8, 0)
         xw_tab = sb("xw_tab", [P, T], U32)
         w_raw = sb("w_raw", [P, PACK, H], F32)
         gs_sb = sb("gs_sb", [P, PACK], F32)
@@ -57,23 +58,25 @@ def tile_picked_daqisendtwo_none_p_kernel(
         d_plane = sb("d_plane", [P, 2, H], U8)
         d_plane_i = d_plane[:].rearrange("p a n -> p (a n)").bitcast(I32)
         nc.vector.memset(ds_tab[:].bitcast(I32), 0)
-        nc.vector.memset(xs_tab[:].bitcast(I32), 0)
+        nc.gpsimd.memset(xs_tab[:, : T // 2].bitcast(I32), 0)
+        nc.vector.memset(xs_tab[:, T // 2 :].bitcast(I32), 0)
         nc.vector.memset(d_plane_i, 0)
 
         w_rows = w1.rearrange("(p j) c -> p j c", j=PACK)
+        x_src = x_words[0].rearrange("p n t -> p (n t)").bitcast(I32)
+        nc.sync.dma_start(xw_tab[:, : T // 4].bitcast(I32), x_src[:, : T // 4])
         nc.sync.dma_start(ka_sb[:], ka)
         nc.sync.dma_start(kb_sb[:], kb)
-        nc.sync.dma_start(w_raw[:, 0:2, :], w_rows[:, 0:2, :])
-        nc.scalar.dma_start(ds_tab[0:P:8, :].bitcast(I32), d_scales[0].bitcast(I32))
         nc.sync.dma_start(offs_sb[:], offs)
-        nc.sync.dma_start(w_raw[:, 2:4, :], w_rows[:, 2:4, :])
-        for i in range(4):
-            nc.scalar.dma_start(xs_tab[i:P:32, :].bitcast(I32), x_scales[0, i:16:4, :].bitcast(I32))
-        nc.sync.dma_start(xw_tab[:].bitcast(I32), x_words[0].rearrange("p n t -> p (n t)").bitcast(I32))
-        nc.sync.dma_start(dw_tab[:].bitcast(I32), d_words[0].rearrange("p n t -> p (n t)").bitcast(I32))
-        nc.gpsimd.dma_start(gs_sb[:], gs.rearrange("(p t) o -> p (t o)", t=PACK))
+        nc.sync.dma_start(ds_tab[0:P:8, :].bitcast(I32), d_scales[0].bitcast(I32))
+        nc.sync.dma_start(gs_sb[:], gs.rearrange("(p t) o -> p (t o)", t=PACK))
         nc.sync.dma_start(n1_sb[:], n1)
+        nc.sync.dma_start(w_raw[:], w_rows)
+        for i in range(4):
+            nc.sync.dma_start(xs_tab[i:P:32, :].bitcast(I32), x_scales[0, i:16:4, :].bitcast(I32))
         nc.sync.dma_start(n2_sb[:], n2)
+        nc.sync.dma_start(xw_tab[:, T // 4 :].bitcast(I32), x_src[:, T // 4 :])
+        nc.sync.dma_start(dw_tab[:].bitcast(I32), d_words[0].rearrange("p n t -> p (n t)").bitcast(I32))
 
         ds_pick = sb("ds_pick", [P, 2, H], U8)
         for a, codes in enumerate((ka_sb, kb_sb)):
@@ -92,16 +95,16 @@ def tile_picked_daqisendtwo_none_p_kernel(
         w_view = w_raw[:].rearrange("p j (m t) -> p m t j", t=PACK)
         w_code, w_plane = [], []
         w_bf = [sb(f"w_bf{u}", [P, 2, P, PACK], BF16) for u in range(2)]
-        nc.scalar.activation(w_bf[0][:].rearrange("p t m j -> p m t j"), w_view[:, :, 0:2, :], COPY)
-        nc.vector.tensor_copy(w_bf[1][:].rearrange("p t m j -> p m t j"), w_view[:, :, 2:4, :])
+        nc.scalar.copy(w_bf[0][:].rearrange("p t m j -> p m t j"), w_view[:, :, 0:2, :])
+        nc.gpsimd.tensor_scalar(w_bf[1][:].rearrange("p t m j -> p m t j"), w_view[:, :, 2:4, :], 1.0, 0.0, MULT, ADD)
         x_plane = sb("x_plane", [P, S], U8)
         nc.vector.tensor_copy(x_plane[:], xs_tab[:].indirect(offs_sb[:]))
-        for u in (1, 0):
+        for u in range(2):
             code = sb(f"w_code{u}", [P, 2 * P], U32)
             plane = sb(f"w_plane{u}", [P, 2 * P], U8)
             nc.vector.quantize_mx(code[:].bitcast(FP8X4), plane[:], w_bf[u][:].rearrange("p t m j -> p (t m j)"))
-            w_code.insert(0, code)
-            w_plane.insert(0, plane)
+            w_code.append(code)
+            w_plane.append(plane)
 
         z_code = sb("z_code", [P, S], U32)
         z_plane = sb("z_plane", [P, S], U8)

@@ -13,7 +13,6 @@ U16 = mybir.dt.uint16
 U8 = mybir.dt.uint8
 FP8X4 = mybir.dt.float8_e4m3fn_x4
 MULT = mybir.AluOpType.mult
-ADD = mybir.AluOpType.add
 MAX = mybir.AluOpType.max
 COPY = mybir.ActivationFunctionType.Copy
 
@@ -69,14 +68,14 @@ def tile_picked_daqisendtwo_none_p_kernel(
         nc.sync.dma_start(kb_sb[:], kb)
         nc.sync.dma_start(offs_sb[:], offs)
         nc.sync.dma_start(ds_tab[0:P:8, :].bitcast(I32), d_scales[0].bitcast(I32))
-        nc.sync.dma_start(gs_sb[:], gs.rearrange("(p t) o -> p (t o)", t=PACK))
-        nc.sync.dma_start(n1_sb[:], n1)
         nc.sync.dma_start(w_raw[:], w_rows)
         for i in range(4):
             nc.sync.dma_start(xs_tab[i:P:32, :].bitcast(I32), x_scales[0, i:16:4, :].bitcast(I32))
-        nc.sync.dma_start(n2_sb[:], n2)
         nc.sync.dma_start(xw_tab[:, T // 4 :].bitcast(I32), x_src[:, T // 4 :])
+        nc.sync.dma_start(gs_sb[:], gs.rearrange("(p t) o -> p (t o)", t=PACK))
         nc.sync.dma_start(dw_tab[:].bitcast(I32), d_words[0].rearrange("p n t -> p (n t)").bitcast(I32))
+        nc.sync.dma_start(n1_sb[:], n1)
+        nc.sync.dma_start(n2_sb[:], n2)
 
         ds_pick = sb("ds_pick", [P, 2, H], U8)
         for a, codes in enumerate((ka_sb, kb_sb)):
@@ -89,29 +88,29 @@ def tile_picked_daqisendtwo_none_p_kernel(
 
         def pick_d_words(c):
             for a, codes in enumerate((ka_sb, kb_sb)):
-                d_code[c, a] = placed(f"d_code{c}{a}", [P, PICK], U32, 2048 + 1024 * a)
+                d_code[c, a] = placed(f"d_code{c}{a}", [P, PICK], U32, 1536 + 1024 * a)
                 nc.vector.tensor_copy(d_code[c, a][:], dw_tab[:].indirect(entries(codes, c * PICK, PICK)))
 
         w_view = w_raw[:].rearrange("p j (m t) -> p m t j", t=PACK)
         w_code, w_plane = [], []
         w_bf = [sb(f"w_bf{u}", [P, 2, P, PACK], BF16) for u in range(2)]
         nc.scalar.copy(w_bf[0][:].rearrange("p t m j -> p m t j"), w_view[:, :, 0:2, :])
-        nc.gpsimd.tensor_scalar(w_bf[1][:].rearrange("p t m j -> p m t j"), w_view[:, :, 2:4, :], 1.0, 0.0, MULT, ADD)
+        nc.vector.tensor_copy(w_bf[1][:].rearrange("p t m j -> p m t j"), w_view[:, :, 2:4, :])
         x_plane = sb("x_plane", [P, S], U8)
         nc.vector.tensor_copy(x_plane[:], xs_tab[:].indirect(offs_sb[:]))
-        for u in range(2):
+        for u in (1, 0):
             code = sb(f"w_code{u}", [P, 2 * P], U32)
             plane = sb(f"w_plane{u}", [P, 2 * P], U8)
             nc.vector.quantize_mx(code[:].bitcast(FP8X4), plane[:], w_bf[u][:].rearrange("p t m j -> p (t m j)"))
-            w_code.append(code)
-            w_plane.append(plane)
+            w_code.insert(0, code)
+            w_plane.insert(0, plane)
 
         z_code = sb("z_code", [P, S], U32)
         z_plane = sb("z_plane", [P, S], U8)
 
         x_codes = []
         for b in range(2):
-            x_codes.append(placed(f"x_code{b}", [P, HALF], U32, 512 * b))
+            x_codes.append(placed(f"x_code{b}", [P, HALF], U32, (1536, 0)[b]))
             nc.vector.tensor_copy(x_codes[b][:], xw_tab[:].indirect(entries(offs_sb, b * HALF, HALF)))
 
         def first_layer(b):
@@ -161,9 +160,11 @@ def tile_picked_daqisendtwo_none_p_kernel(
                 nc.scalar.activation(sent[r][a][:].indirect(entries(places, first, count)), h_sb[r][:, cols], COPY)
 
         def finish(r):
+            parts = ((nc.sync, slice(0, HALF)), (nc.scalar, slice(HALF, S))) if r == 3 else ((nc.sync, slice(0, S)),)
             res = sb(f"res{r}", [P, S], F32)
-            nc.vector.tensor_tensor(res[:], sent[r][0][:, :S], sent[r][1][:, :S], MAX)
-            nc.sync.dma_start(out[r * P : (r + 1) * P, :], res[:])
+            for queue, cols in parts:
+                nc.vector.tensor_tensor(res[:, cols], sent[r][0][:, cols], sent[r][1][:, cols], MAX)
+                queue.dma_start(out[r * P : (r + 1) * P, cols], res[:, cols])
 
         first_layer(0)
         pick_d_words(0)

from contextlib import ExitStack

import concourse.mybir as mybir

K, T, S, H, G = 512, 2048, 256, 512, 2048
FLOPS = 2 * K * H * S * 3

F32 = mybir.dt.float32
BF16 = mybir.dt.bfloat16
I32 = mybir.dt.int32
U32 = mybir.dt.uint32
U16 = mybir.dt.uint16
U8 = mybir.dt.uint8
FP8X4 = mybir.dt.float8_e4m3fn_x4
MULT = mybir.AluOpType.mult
MAX = mybir.AluOpType.max
COPY = mybir.ActivationFunctionType.Copy

P = 128
PACK = 4
LIST = 16
HALF = S // 2
PICK = 256
WIDE = 2 * S


def tile_picked_daqisendtwo_none_p_kernel(
    tc, x_words, x_scales, w1, gs, d_words, d_scales, offs, ka, kb, n1, n2, out
):
    nc = tc.nc
    with ExitStack() as ctx:
        keep = ctx.enter_context(tc.tile_pool(name="keep", bufs=1))
        reuse = ctx.enter_context(tc.tile_pool(name="reuse", bufs=1))
        psum = ctx.enter_context(tc.psum_pool(name="psum", bufs=1))

        def sb(name, shape, dtype):
            return keep.tile(shape, dtype, name=name, align_bytes=64)

        def placed(name, shape, dtype, at):
            return reuse.tile(shape, dtype, name=name, align_bytes=64, offset=at)

        def entries(tile, first, count):
            return tile[:, first // LIST : (first + count) // LIST]

        ka_sb = sb("ka_sb", [P, H // LIST], U16)
        kb_sb = sb("kb_sb", [P, H // LIST], U16)
        offs_sb = sb("offs_sb", [P, S // LIST], U16)
        n1_sb = sb("n1_sb", [P, S // LIST], U16)
        n2_sb = sb("n2_sb", [P, S // LIST], U16)
        ds_tab = sb("ds_tab", [P, G], U8)
        dw_tab = sb("dw_tab", [P, G], U32)
        xs_tab = placed("xs_tab", [P, T], U8, 0)
        xw_tab = sb("xw_tab", [P, T], U32)
        w_raw = sb("w_raw", [P, PACK, H], F32)
        gs_sb = sb("gs_sb", [P, PACK], F32)

        d_plane = sb("d_plane", [P, 2, H], U8)
        d_plane_i = d_plane[:].rearrange("p a n -> p (a n)").bitcast(I32)
        nc.vector.memset(ds_tab[:].bitcast(I32), 0)
        nc.gpsimd.memset(xs_tab[:, : T // 2].bitcast(I32), 0)
        nc.vector.memset(xs_tab[:, T // 2 :].bitcast(I32), 0)
        nc.vector.memset(d_plane_i, 0)

        w_rows = w1.rearrange("(p j) c -> p j c", j=PACK)
        x_src = x_words[0].rearrange("p n t -> p (n t)").bitcast(I32)
        nc.sync.dma_start(xw_tab[:, : T // 4].bitcast(I32), x_src[:, : T // 4])
        nc.sync.dma_start(ka_sb[:], ka)
        nc.sync.dma_start(kb_sb[:], kb)
        nc.sync.dma_start(offs_sb[:], offs)
        nc.sync.dma_start(ds_tab[0:P:8, :].bitcast(I32), d_scales[0].bitcast(I32))
        nc.sync.dma_start(w_raw[:], w_rows)
        for i in range(4):
            nc.sync.dma_start(xs_tab[i:P:32, :].bitcast(I32), x_scales[0, i:16:4, :].bitcast(I32))
        nc.sync.dma_start(xw_tab[:, T // 4 :].bitcast(I32), x_src[:, T // 4 :])
        nc.sync.dma_start(gs_sb[:], gs.rearrange("(p t) o -> p (t o)", t=PACK))
        nc.sync.dma_start(dw_tab[:].bitcast(I32), d_words[0].rearrange("p n t -> p (n t)").bitcast(I32))
        nc.sync.dma_start(n1_sb[:], n1)
        nc.sync.dma_start(n2_sb[:], n2)

        ds_pick = sb("ds_pick", [P, 2, H], U8)
        for a, codes in enumerate((ka_sb, kb_sb)):
            nc.vector.tensor_copy(ds_pick[:, a, :], ds_tab[:].indirect(codes[:]))
        ds_pick_i = ds_pick[:].rearrange("p a n -> p (a n)").bitcast(I32)
        for i in range(4):
            nc.sync.dma_start(d_plane_i[i:P:32, :], ds_pick_i[8 * i : P : 32, :])

        d_code = {}

        def pick_d_words(c):
            for a, codes in enumerate((ka_sb, kb_sb)):
                d_code[c, a] = placed(f"d_code{c}{a}", [P, PICK], U32, 1536 + 1024 * a)
                nc.vector.tensor_copy(d_code[c, a][:], dw_tab[:].indirect(entries(codes, c * PICK, PICK)))

        w_view = w_raw[:].rearrange("p j (m t) -> p m t j", t=PACK)
        w_code, w_plane = [], []
        w_bf = [sb(f"w_bf{u}", [P, 2, P, PACK], BF16) for u in range(2)]
        nc.scalar.copy(w_bf[0][:].rearrange("p t m j -> p m t j"), w_view[:, :, 0:2, :])
        nc.vector.tensor_copy(w_bf[1][:].rearrange("p t m j -> p m t j"), w_view[:, :, 2:4, :])
        x_plane = sb("x_plane", [P, S], U8)
        nc.vector.tensor_copy(x_plane[:], xs_tab[:].indirect(offs_sb[:]))
        for u in (1, 0):
            code = sb(f"w_code{u}", [P, 2 * P], U32)
            plane = sb(f"w_plane{u}", [P, 2 * P], U8)
            nc.vector.quantize_mx(code[:].bitcast(FP8X4), plane[:], w_bf[u][:].rearrange("p t m j -> p (t m j)"))
            w_code.insert(0, code)
            w_plane.insert(0, plane)

        z_code = sb("z_code", [P, S], U32)
        z_plane = sb("z_plane", [P, S], U8)

        x_codes = []
        for b in range(2):
            x_codes.append(placed(f"x_code{b}", [P, HALF], U32, (1536, 0)[b]))
            nc.vector.tensor_copy(x_codes[b][:], xw_tab[:].indirect(entries(offs_sb, b * HALF, HALF)))

        def first_layer(b):
            cols = slice(b * HALF, (b + 1) * HALF)
            x_code = x_codes[b]
            y = psum.tile([P, PACK, HALF], F32, name=f"y{b}", tag=f"bank_y{b}")
            for t in range(PACK):
                m = slice((t % 2) * P, (t % 2 + 1) * P)
                nc.tensor.matmul_mx(
                    y[:, t, :],
                    lhsT=w_code[t // 2][:, m].bitcast(FP8X4),
                    lhsT_scale=w_plane[t // 2][:, m],
                    rhs=x_code[:].bitcast(FP8X4),
                    rhs_scale=x_plane[:, cols],
                    start=True,
                    stop=True,
                )
            z_bf = placed(f"z_bf{b}", [P, HALF, PACK], BF16, (2048 + 512, 4096)[b])
            nc.vector.tensor_tensor(
                z_bf[:],
                y[:].rearrange("p t n -> p n t"),
                gs_sb[:].unsqueeze(1).to_broadcast([P, HALF, PACK]),
                MULT,
            )
            nc.vector.quantize_mx(z_code[:, cols].bitcast(FP8X4), z_plane[:, cols], z_bf[:].rearrange("p n t -> p (n t)"))

        h_sb = [sb(f"h_sb{r}", [P, S], F32) for r in range(4)]
        sent = [[sb(f"sent{r}{a}", [P, WIDE], F32) for a in range(2)] for r in range(4)]

        def second_layer(r, first, count):
            cols = slice(first, first + count)
            c, m = r // 2, slice((r % 2) * P, (r % 2 + 1) * P)
            tag = "bank_y1" if (r, first) == (0, 0) else f"bank{r}_{first}"
            acc = psum.tile([P, count], F32, name=f"acc{r}_{first}", tag=tag)
            for a in range(2):
                nc.tensor.matmul_mx(
                    acc[:],
                    lhsT=d_code[c, a][:, m].bitcast(FP8X4),
                    lhsT_scale=d_plane[:, a, r * P : (r + 1) * P],
                    rhs=z_code[:, cols].bitcast(FP8X4),
                    rhs_scale=z_plane[:, cols],
                    start=(a == 0),
                    stop=(a == 1),
                )
            nc.vector.tensor_scalar_mul(h_sb[r][:, cols], acc[:], 0.0625)
            for a, places in enumerate((n1_sb, n2_sb)):
                nc.scalar.activation(sent[r][a][:].indirect(entries(places, first, count)), h_sb[r][:, cols], COPY)

        def finish(r):
            parts = ((nc.sync, slice(0, HALF)), (nc.scalar, slice(HALF, S))) if r == 3 else ((nc.sync, slice(0, S)),)
            res = sb(f"res{r}", [P, S], F32)
            for queue, cols in parts:
                nc.vector.tensor_tensor(res[:, cols], sent[r][0][:, cols], sent[r][1][:, cols], MAX)
                queue.dma_start(out[r * P : (r + 1) * P, cols], res[:, cols])

        first_layer(0)
        pick_d_words(0)
        second_layer(0, 0, HALF)
        second_layer(1, 0, HALF)
        first_layer(1)
        second_layer(0, HALF, HALF)
        second_layer(1, HALF, HALF)
        pick_d_words(1)
        finish(0)
        second_layer(2, 0, S)
        finish(1)
        second_layer(3, 0, S)
        finish(2)
        finish(3)
